import numpy as np
import ml_dtypes


def mxq(x, axis, fmt="e4m3"):
    dtype, down = {"e4m3": (ml_dtypes.float8_e4m3fn, 7), "e5m2": (ml_dtypes.float8_e5m2, 14)}[fmt]
    v = np.moveaxis(np.asarray(x, np.float32).astype(ml_dtypes.bfloat16).astype(np.float64), axis, -1)
    blocks = v.reshape(v.shape[:-1] + (-1, 32))
    amax = np.abs(blocks).max(-1, keepdims=True)
    byte = np.maximum(np.where(amax > 0, np.frexp(amax)[1] - 1 + 127, 0) - down, 1)
    scale = np.exp2(byte - 127.0)
    codes = (blocks / scale).astype(np.float32).astype(dtype).astype(np.float64)
    return np.moveaxis((codes * scale).reshape(v.shape), -1, axis)


WIDE = False


def mx_kscale(k):
    if not WIDE:
        return np.ones(k)
    levels = np.array([10, -10, 5, -5, 0])
    if k % 512:
        return np.exp2(np.random.permutation(np.resize(levels, k // 32))).repeat(32)
    a = np.empty((k // 512, 16))
    for p in range(k // 512):
        a[p, :8] = np.random.permutation(np.resize(levels, 8))
        for g in range(8):
            far = levels[np.abs(levels - a[p, g]) >= 10]
            a[p, g + 8] = far[np.random.randint(len(far))]
    return np.exp2(a.ravel()).repeat(32)


BF16 = ml_dtypes.bfloat16


def bf(x):
    return np.asarray(x, np.float32).astype(BF16)


def f64(x):
    return np.asarray(x).astype(np.float64)


E2M1 = np.array([0.0, 0.5, 1.0, 1.5, 2.0, 3.0, 4.0, 6.0, -0.0, -0.5, -1.0, -1.5, -2.0, -3.0, -4.0, -6.0])


def pack_weight(w, fmt):
    k, n = w.shape
    w = f64(bf(w)).reshape(k // 32, 32, n)
    amax = np.abs(w).max(1)
    if fmt == "e4m3":
        byte = np.frexp(amax)[1] - 1 + 127 - 7
    else:
        mant, ex = np.frexp(amax / 6.0)
        byte = np.where(mant > 0.5, ex, ex - 1) + 127
    byte = np.clip(np.where(amax > 0, byte, 1), 1, 254)
    scaled = (w * np.exp2(127.0 - byte)[:, None, :]).reshape(k, n).astype(np.float32)
    by_word = np.ascontiguousarray(scaled.reshape(k // 512, 128, 4, n).transpose(0, 1, 3, 2))
    if fmt == "e4m3":
        words = by_word.astype(ml_dtypes.float8_e4m3fn).view(np.uint8)
    else:
        c = by_word.astype(ml_dtypes.float4_e2m1fn).view(np.uint8) & 0xF
        words = c[..., 0::2] | (c[..., 1::2] << 4)
    return np.ascontiguousarray(words), np.ascontiguousarray(byte.astype(np.uint8).reshape(k // 512, 16, n))


def unpack_weight(words, scales, fmt):
    g, p, n, _ = words.shape
    if fmt == "e4m3":
        vals = np.ascontiguousarray(words).view(ml_dtypes.float8_e4m3fn).astype(np.float64)
    else:
        nib = np.empty((g, p, n, 4), np.uint8)
        nib[..., 0::2] = words & 0xF
        nib[..., 1::2] = words >> 4
        vals = E2M1[nib]
    vals = vals * np.repeat(np.exp2(scales.astype(np.float64) - 127.0), 8, axis=1)[..., None]
    return vals.transpose(0, 1, 3, 2).reshape(g * 512, n)
def pack4(w):
    words, scales = pack_weight(w, "e2m1")
    return words.reshape(words.shape[0], 128, -1), scales


def unpack4(words, scales):
    return unpack_weight(words.reshape(words.shape[0], 128, -1, 2), scales, "e2m1")


M, K, KC, N = 1024, 1536, 512, 1024


def setup_inputs():
    s = mx_kscale(K)
    gr = np.random.standard_normal((K, N)) / np.sqrt(K) / s[:, None]
    gz = np.random.standard_normal((K, N)) / np.sqrt(K) / s[:, None]
    gr_words, gr_scales = pack_weight(gr, "e4m3")
    gz_words, gz_scales = pack4(gz)
    return {"coil": bf(np.random.standard_normal((M, KC)) * s[:KC]),
            "plasma": bf(np.random.standard_normal((M, K - KC)) * s[KC:]),
            "gpsi": bf(np.random.standard_normal((K, N)) / np.sqrt(K) / s[:, None]),
            "gr_words": gr_words,
            "gr_scales": gr_scales,
            "gz_words": gz_words,
            "gz_scales": gz_scales,
            "dr": bf(0.6 * np.random.standard_normal((M, N))),
            "dz": bf(0.6 * np.random.standard_normal((M, N)))}


def reference(coil, plasma, gpsi, gr_words, gr_scales, gz_words, gz_scales, dr, dz):
    cur = mxq(np.concatenate([f64(coil), f64(plasma)], axis=1), 1, "e4m3")
    psi = cur @ mxq(f64(gpsi), 0, "e4m3")
    psi_r = cur @ unpack_weight(gr_words, gr_scales, "e4m3")
    psi_z = cur @ unpack4(gz_words, gz_scales)
    return psi + f64(dr) * psi_r + f64(dz) * psi_z

@@ -1,0 +1,277 @@
+from contextlib import ExitStack
+
+import concourse.mybir as mybir
+from concourse.masks import make_identity
+
+M, K, KC, N = 1024, 1536, 512, 1024
+FLOPS = 3 * 2 * M * K * N
+
+F32 = mybir.dt.float32
+BF16 = mybir.dt.bfloat16
+I32 = mybir.dt.int32
+U32 = mybir.dt.uint32
+U8 = mybir.dt.uint8
+FP8X4 = mybir.dt.float8_e4m3fn_x4
+FP4X4 = mybir.dt.float4_e2m1fn_x4
+ADD = mybir.AluOpType.add
+MULT = mybir.AluOpType.mult
+
+P = 128
+PACK = 4
+K_PASS = P * PACK
+G = K // K_PASS
+TILES = M // P
+PAIRS = TILES // 2
+NH = 512
+HALVES = N // NH
+BANKS = 8
+ALIGN = 256
+
+
+def tile_moved_point_flux_s10_kernel(
+    tc, coil, plasma, gpsi, gr_words, gr_scales, gz_words, gz_scales, dr, dz, out
+):
+    nc = tc.nc
+    coil_v = coil.rearrange("(p t) k -> p t k", t=TILES)
+    plasma_v = plasma.rearrange("(p t) k -> p t k", t=TILES)
+    dr_v = dr.rearrange("(p t) n -> p t n", t=TILES)
+    dz_v = dz.rearrange("(p t) n -> p t n", t=TILES)
+    out_v = out.rearrange("(p t) n -> p t n", t=TILES)
+    gpsi_v = gpsi.rearrange("(g p j) n -> g p j n", p=P, j=PACK)
+    gr_v = gr_words.rearrange("g p n t -> p g (n t)").bitcast(I32)
+    gz_v = gz_words.rearrange("g p b -> p g b").bitcast(I32)
+    grs_v = gr_scales.bitcast(I32).rearrange("g (q r) w -> r q g w", r=4)
+    gzs_v = gz_scales.bitcast(I32).rearrange("g (q r) w -> r q g w", r=4)
+
+    with ExitStack() as ctx:
+        keep = ctx.enter_context(tc.tile_pool(name="keep", bufs=1))
+        ring = ctx.enter_context(tc.tile_pool(name="ring", bufs=4))
+        psum = ctx.enter_context(tc.psum_pool(name="psum", bufs=1))
+        ctx.enter_context(tc.manual_schedule())
+
+        def kept(name, shape, dtype):
+            return keep.tile(shape, dtype, name=name, align_bytes=ALIGN)
+
+        bank_count = [0]
+
+        def next_bank():
+            index = bank_count[0] % BANKS
+            bank_count[0] += 1
+            return psum.tile([P, NH], F32, name="bank%d" % index)
+
+        chunks = [(j, x) for j in range(PAIRS) for x in range(3)]
+        raw_i = {c: kept("raw_i%d%d" % c, [P, 2, K_PASS], BF16) for c in chunks}
+        i_codes = {c: kept("i_codes%d%d" % c, [P, 2, P], U32) for c in chunks}
+        i_scales = {c: kept("i_scales%d%d" % c, [P, 2, P], U8) for c in chunks}
+        z_codes = [kept("z_codes%d" % h, [P, G, 2 * NH], U8) for h in range(HALVES)]
+        z_scales = [kept("z_scales%d" % h, [P, G, NH], U8) for h in range(HALVES)]
+        r_codes = [kept("r_codes%d" % h, [P, G, NH], U32) for h in range(HALVES)]
+        r_scales = kept("r_scales", [P, G, N], U8)
+        raw_g = [kept("raw_g%d" % g, [P, PACK, N], BF16) for g in range(G)]
+        g_codes = {(g, h): kept("g_codes%d%d" % (g, h), [P, NH], U32) for g in range(G) for h in range(HALVES)}
+        g_scales = {(g, h): kept("g_scales%d%d" % (g, h), [P, NH], U8) for g in range(G) for h in range(HALVES)}
+        dr_sb = [kept("dr%d" % j, [P, 2, N], BF16) for j in range(PAIRS)]
+        dz_sb = [kept("dz%d" % j, [P, 2, N], BF16) for j in range(PAIRS)]
+        acc = {(m, h): kept("acc%d%d" % (m, h), [P, NH], F32) for m in range(TILES) for h in range(HALVES)}
+        ident = kept("ident", [P, P], F32)
+        warm = kept("warm", [P, 16], F32)
+
+        def load_chunk(j, x):
+            if x == 0:
+                src = coil_v[:, 2 * j : 2 * j + 2, :]
+            else:
+                src = plasma_v[:, 2 * j + x - 1, :].rearrange("p (s k) -> p s k", s=2)
+            nc.sync.dma_start(out=raw_i[j, x][:], in_=src)
+
+        def load_pair(j):
+            for x in range(3):
+                load_chunk(j, x)
+
+        def load_z(h):
+            words = NH // 4
+            for r in range(4):
+                nc.sync.dma_start(
+                    out=z_scales[h][r:P:32, :, :].bitcast(I32),
+                    in_=gzs_v[r][:, :, h * words : (h + 1) * words],
+                )
+            words = NH // 2
+            nc.sync.dma_start(out=z_codes[h][:].bitcast(I32), in_=gz_v[:, :, h * words : (h + 1) * words])
+
+        def load_r_scales():
+            for r in range(4):
+                nc.sync.dma_start(out=r_scales[r:P:32, :, :].bitcast(I32), in_=grs_v[r])
+
+        def load_r(h):
+            nc.sync.dma_start(out=r_codes[h][:].bitcast(I32), in_=gr_v[:, :, h * NH : (h + 1) * NH])
+
+        def load_g(g):
+            nc.sync.dma_start(out=raw_g[g][:], in_=gpsi_v[g])
+
+        def load_d(dst, src, j):
+            nc.sync.dma_start(out=dst[j][:], in_=src[:, 2 * j : 2 * j + 2, :])
+
+        sorted_words = {}
+        turned = {}
+        grouped_i = {}
+        grouped_g = {}
+        sums = {}
+        products = {}
+
+        def words_of(j, x):
+            return raw_i[j, x][:].rearrange("p s k -> p (s k)").bitcast(F32)
+
+        def sort_words(j, x):
+            dst = ring.tile([P, 2, 2, P], F32, name="sorted_words")
+            nc.scalar.copy(out=dst[:], in_=words_of(j, x).rearrange("p (s q u) -> p s u q", s=2, u=2))
+            sorted_words[j, x] = dst
+
+        def transpose_chunk(j, x):
+            bank = next_bank()
+            for s in range(2):
+                for u in range(2):
+                    if (j, x) in sorted_words:
+                        src = sorted_words[j, x][:, s, u, :]
+                    else:
+                        src = words_of(j, x)[:, 2 * P * s + u : 2 * P * (s + 1) : 2]
+                    col = (2 * s + u) * P
+                    nc.tensor.transpose(bank[:, col : col + P], src, ident[:])
+            turned[j, x] = bank
+
+        def evacuate(j, x):
+            dst = ring.tile([P, 2 * P * PACK], BF16, name="grouped_i", align_bytes=ALIGN)
+            nc.scalar.copy(
+                out=dst[:].bitcast(F32).rearrange("p (s r u) -> p s r u", s=2, u=2),
+                in_=turned[j, x][:].rearrange("p (s u r) -> p s r u", s=2, u=2),
+            )
+            grouped_i[j, x] = dst
+
+        def quantize_i(j, x):
+            nc.vector.quantize_mx(
+                out=i_codes[j, x][:].rearrange("p s r -> p (s r)").bitcast(FP8X4),
+                scales=i_scales[j, x][:].rearrange("p s r -> p (s r)"),
+                in_=grouped_i[j, x][:],
+            )
+
+        def interleave_g(g, h):
+            dst = ring.tile([P, NH * PACK], BF16, name="grouped_g", bufs=3, align_bytes=ALIGN)
+            nc.scalar.copy(
+                out=dst[:].rearrange("p (c i t) -> p c t i", i=4, t=PACK),
+                in_=raw_g[g][:, :, h * NH : (h + 1) * NH].rearrange("p t (c i) -> p c t i", i=4),
+            )
+            grouped_g[g, h] = dst
+
+        def quantize_g(g, h):
+            nc.vector.quantize_mx(out=g_codes[g, h][:].bitcast(FP8X4), scales=g_scales[g, h][:], in_=grouped_g[g, h][:])
+
+        def moving(w, g, h):
+            if w == "z":
+                return z_codes[h][:, g, :].bitcast(FP4X4), z_scales[h][:, g, :]
+            if w == "r":
+                return r_codes[h][:, g, :].bitcast(FP8X4), r_scales[:, g, h * NH : (h + 1) * NH]
+            return g_codes[g, h][:].bitcast(FP8X4), g_scales[g, h][:]
+
+        def multiply(w, m, h, cols=slice(0, NH)):
+            bank = next_bank()
+            j, t = divmod(m, 2)
+            for g in range(G):
+                chunk, s = ((j, 0), t) if g == 0 else ((j, 1 + t), g - 1)
+                codes, scales = moving(w, g, h)
+                nc.tensor.matmul_mx(
+                    out=bank[:, cols],
+                    lhsT=i_codes[chunk][:, s, :].bitcast(FP8X4),
+                    lhsT_scale=i_scales[chunk][:, s, :],
+                    rhs=codes[:, cols],
+                    rhs_scale=scales[:, cols],
+                    start=(g == 0),
+                    stop=(g == G - 1),
+                )
+            sums[w, m, h] = bank
+
+        def shift(d_sb, m, h):
+            return d_sb[m // 2][:, m % 2, h * NH : (h + 1) * NH]
+
+        def finish_z(m, h):
+            nc.vector.tensor_tensor(out=acc[m, h][:], in0=sums["z", m, h][:], in1=shift(dz_sb, m, h), op=MULT)
+
+        def finish_r(m, h):
+            prod = ring.tile([P, NH], F32, name="product", bufs=9)
+            nc.vector.tensor_tensor(out=prod[:], in0=sums["r", m, h][:], in1=shift(dr_sb, m, h), op=MULT)
+            nc.gpsimd.tensor_tensor(out=acc[m, h][:], in0=acc[m, h][:], in1=prod[:], op=ADD)
+
+        def finish_p(m, h, cols=slice(0, NH)):
+            part = acc[m, h][:, cols]
+            nc.vector.tensor_tensor(out=part, in0=sums["p", m, h][:, cols], in1=part, op=ADD)
+            nc.sync.dma_start(out=out_v[:, m, h * NH + cols.start : h * NH + cols.stop], in_=part)
+
+        nc.vector.memset(warm[:], 0.0)
+        nc.vector.memset(z_scales[0][:].bitcast(I32), 0)
+        nc.vector.memset(z_scales[1][:].bitcast(I32), 0)
+        nc.vector.memset(r_scales[:].bitcast(I32), 0)
+        nc.scalar.copy(out=warm[:, 8:9], in_=warm[:, 0:1])
+        make_identity(nc, ident[:])
+
+        load_pair(0)
+        load_z(0)
+        load_pair(1)
+        load_z(1)
+        load_d(dz_sb, dz_v, 0)
+        load_pair(2)
+        load_d(dz_sb, dz_v, 1)
+        load_pair(3)
+        load_d(dz_sb, dz_v, 2)
+        load_g(0)
+        load_d(dz_sb, dz_v, 3)
+        load_r_scales()
+        load_r(0)
+        load_d(dr_sb, dr_v, 0)
+        load_g(1)
+        load_d(dr_sb, dr_v, 1)
+        load_d(dr_sb, dr_v, 2)
+        load_r(1)
+        load_g(2)
+        load_d(dr_sb, dr_v, 3)
+
+        for j in range(PAIRS):
+            for x in range(3):
+                transpose_chunk(j, x)
+            for x in range(3):
+                evacuate(j, x)
+            if j + 1 < PAIRS:
+                for x in range(3):
+                    sort_words(j + 1, x)
+            for x in range(3):
+                quantize_i(j, x)
+            if j == 1:
+                finish_z(0, 0)
+                finish_z(1, 0)
+            if j > 0:
+                for m in (2 * j - 2, 2 * j - 1):
+                    multiply("z", m, 1)
+                    finish_z(m, 1)
+            for m in (2 * j, 2 * j + 1):
+                multiply("z", m, 0)
+                if j > 0:
+                    finish_z(m, 0)
+        interleave_g(0, 0)
+        quantize_g(0, 0)
+        for m in (TILES - 2, TILES - 1):
+            multiply("z", m, 1)
+            finish_z(m, 1)
+
+        after_r = {1: (0, 1), 4: (1, 0), 5: (1, 1), 11: (2, 0)}
+        units = [(m, h) for h in range(HALVES) for m in range(TILES)]
+        for index, (m, h) in enumerate(units):
+            multiply("r", m, h)
+            finish_r(m, h)
+            if index in after_r:
+                interleave_g(*after_r[index])
+                quantize_g(*after_r[index])
+        for index, (m, h) in enumerate(units[:-1]):
+            multiply("p", m, h)
+            finish_p(m, h)
+            if index == 2:
+                interleave_g(2, 1)
+                quantize_g(2, 1)
+        for cols in (slice(0, NH // 2), slice(NH // 2, NH)):
+            multiply("p", TILES - 1, HALVES - 1, cols)
+            finish_p(TILES - 1, HALVES - 1, cols)

@@ -220,16 +220,16 @@ def tile_moved_point_flux_s10_kernel(
         load_pair(3)
         load_d(dz_sb, dz_v, 2)
         load_g(0)
-        load_d(dz_sb, dz_v, 3)
         load_r_scales()
+        load_d(dz_sb, dz_v, 3)
         load_r(0)
         load_d(dr_sb, dr_v, 0)
         load_g(1)
         load_d(dr_sb, dr_v, 1)
         load_d(dr_sb, dr_v, 2)
         load_r(1)
-        load_g(2)
         load_d(dr_sb, dr_v, 3)
+        load_g(2)
 
         for j in range(PAIRS):
             for x in range(3):
@@ -258,7 +258,7 @@ def tile_moved_point_flux_s10_kernel(
             multiply("z", m, 1)
             finish_z(m, 1)
 
-        after_r = {1: (0, 1), 4: (1, 0), 5: (1, 1), 11: (2, 0)}
+        after_r = {1: (0, 1), 4: (1, 0), 7: (1, 1), 11: (2, 0)}
         units = [(m, h) for h in range(HALVES) for m in range(TILES)]
         for index, (m, h) in enumerate(units):
             multiply("r", m, h)
@@ -269,7 +269,7 @@ def tile_moved_point_flux_s10_kernel(
         for index, (m, h) in enumerate(units[:-1]):
             multiply("p", m, h)
             finish_p(m, h)
-            if index == 2:
+            if index == 1:
                 interleave_g(2, 1)
                 quantize_g(2, 1)
         for cols in (slice(0, NH // 2), slice(NH // 2, NH)):

from contextlib import ExitStack

import concourse.mybir as mybir
from concourse.masks import make_identity

M, K, KC, N = 1024, 1536, 512, 1024
FLOPS = 3 * 2 * M * K * N

F32 = mybir.dt.float32
BF16 = mybir.dt.bfloat16
I32 = mybir.dt.int32
U32 = mybir.dt.uint32
U8 = mybir.dt.uint8
FP8X4 = mybir.dt.float8_e4m3fn_x4
FP4X4 = mybir.dt.float4_e2m1fn_x4
ADD = mybir.AluOpType.add
MULT = mybir.AluOpType.mult

P = 128
PACK = 4
K_PASS = P * PACK
G = K // K_PASS
TILES = M // P
PAIRS = TILES // 2
NH = 512
HALVES = N // NH
BANKS = 8
ALIGN = 256


def tile_moved_point_flux_s10_kernel(
    tc, coil, plasma, gpsi, gr_words, gr_scales, gz_words, gz_scales, dr, dz, out
):
    nc = tc.nc
    coil_v = coil.rearrange("(p t) k -> p t k", t=TILES)
    plasma_v = plasma.rearrange("(p t) k -> p t k", t=TILES)
    dr_v = dr.rearrange("(p t) n -> p t n", t=TILES)
    dz_v = dz.rearrange("(p t) n -> p t n", t=TILES)
    out_v = out.rearrange("(p t) n -> p t n", t=TILES)
    gpsi_v = gpsi.rearrange("(g p j) n -> g p j n", p=P, j=PACK)
    gr_v = gr_words.rearrange("g p n t -> p g (n t)").bitcast(I32)
    gz_v = gz_words.rearrange("g p b -> p g b").bitcast(I32)
    grs_v = gr_scales.bitcast(I32).rearrange("g (q r) w -> r q g w", r=4)
    gzs_v = gz_scales.bitcast(I32).rearrange("g (q r) w -> r q g w", r=4)

    with ExitStack() as ctx:
        keep = ctx.enter_context(tc.tile_pool(name="keep", bufs=1))
        ring = ctx.enter_context(tc.tile_pool(name="ring", bufs=4))
        psum = ctx.enter_context(tc.psum_pool(name="psum", bufs=1))
        ctx.enter_context(tc.manual_schedule())

        def kept(name, shape, dtype):
            return keep.tile(shape, dtype, name=name, align_bytes=ALIGN)

        bank_count = [0]

        def next_bank():
            index = bank_count[0] % BANKS
            bank_count[0] += 1
            return psum.tile([P, NH], F32, name="bank%d" % index)

        chunks = [(j, x) for j in range(PAIRS) for x in range(3)]
        raw_i = {c: kept("raw_i%d%d" % c, [P, 2, K_PASS], BF16) for c in chunks}
        i_codes = {c: kept("i_codes%d%d" % c, [P, 2, P], U32) for c in chunks}
        i_scales = {c: kept("i_scales%d%d" % c, [P, 2, P], U8) for c in chunks}
        z_codes = [kept("z_codes%d" % h, [P, G, 2 * NH], U8) for h in range(HALVES)]
        z_scales = [kept("z_scales%d" % h, [P, G, NH], U8) for h in range(HALVES)]
        r_codes = [kept("r_codes%d" % h, [P, G, NH], U32) for h in range(HALVES)]
        r_scales = kept("r_scales", [P, G, N], U8)
        raw_g = [kept("raw_g%d" % g, [P, PACK, N], BF16) for g in range(G)]
        g_codes = {(g, h): kept("g_codes%d%d" % (g, h), [P, NH], U32) for g in range(G) for h in range(HALVES)}
        g_scales = {(g, h): kept("g_scales%d%d" % (g, h), [P, NH], U8) for g in range(G) for h in range(HALVES)}
        dr_sb = [kept("dr%d" % j, [P, 2, N], BF16) for j in range(PAIRS)]
        dz_sb = [kept("dz%d" % j, [P, 2, N], BF16) for j in range(PAIRS)]
        acc = {(m, h): kept("acc%d%d" % (m, h), [P, NH], F32) for m in range(TILES) for h in range(HALVES)}
        ident = kept("ident", [P, P], F32)
        warm = kept("warm", [P, 16], F32)

        def load_chunk(j, x):
            if x == 0:
                src = coil_v[:, 2 * j : 2 * j + 2, :]
            else:
                src = plasma_v[:, 2 * j + x - 1, :].rearrange("p (s k) -> p s k", s=2)
            nc.sync.dma_start(out=raw_i[j, x][:], in_=src)

        def load_pair(j):
            for x in range(3):
                load_chunk(j, x)

        def load_z(h):
            words = NH // 4
            for r in range(4):
                nc.sync.dma_start(
                    out=z_scales[h][r:P:32, :, :].bitcast(I32),
                    in_=gzs_v[r][:, :, h * words : (h + 1) * words],
                )
            words = NH // 2
            nc.sync.dma_start(out=z_codes[h][:].bitcast(I32), in_=gz_v[:, :, h * words : (h + 1) * words])

        def load_r_scales():
            for r in range(4):
                nc.sync.dma_start(out=r_scales[r:P:32, :, :].bitcast(I32), in_=grs_v[r])

        def load_r(h):
            nc.sync.dma_start(out=r_codes[h][:].bitcast(I32), in_=gr_v[:, :, h * NH : (h + 1) * NH])

        def load_g(g):
            nc.sync.dma_start(out=raw_g[g][:], in_=gpsi_v[g])

        def load_d(dst, src, j):
            nc.sync.dma_start(out=dst[j][:], in_=src[:, 2 * j : 2 * j + 2, :])

        sorted_words = {}
        turned = {}
        grouped_i = {}
        grouped_g = {}
        sums = {}
        products = {}

        def words_of(j, x):
            return raw_i[j, x][:].rearrange("p s k -> p (s k)").bitcast(F32)

        def sort_words(j, x):
            dst = ring.tile([P, 2, 2, P], F32, name="sorted_words")
            nc.scalar.copy(out=dst[:], in_=words_of(j, x).rearrange("p (s q u) -> p s u q", s=2, u=2))
            sorted_words[j, x] = dst

        def transpose_chunk(j, x):
            bank = next_bank()
            for s in range(2):
                for u in range(2):
                    if (j, x) in sorted_words:
                        src = sorted_words[j, x][:, s, u, :]
                    else:
                        src = words_of(j, x)[:, 2 * P * s + u : 2 * P * (s + 1) : 2]
                    col = (2 * s + u) * P
                    nc.tensor.transpose(bank[:, col : col + P], src, ident[:])
            turned[j, x] = bank

        def evacuate(j, x):
            dst = ring.tile([P, 2 * P * PACK], BF16, name="grouped_i", align_bytes=ALIGN)
            nc.scalar.copy(
                out=dst[:].bitcast(F32).rearrange("p (s r u) -> p s r u", s=2, u=2),
                in_=turned[j, x][:].rearrange("p (s u r) -> p s r u", s=2, u=2),
            )
            grouped_i[j, x] = dst

        def quantize_i(j, x):
            nc.vector.quantize_mx(
                out=i_codes[j, x][:].rearrange("p s r -> p (s r)").bitcast(FP8X4),
                scales=i_scales[j, x][:].rearrange("p s r -> p (s r)"),
                in_=grouped_i[j, x][:],
            )

        def interleave_g(g, h):
            dst = ring.tile([P, NH * PACK], BF16, name="grouped_g", bufs=3, align_bytes=ALIGN)
            nc.scalar.copy(
                out=dst[:].rearrange("p (c i t) -> p c t i", i=4, t=PACK),
                in_=raw_g[g][:, :, h * NH : (h + 1) * NH].rearrange("p t (c i) -> p c t i", i=4),
            )
            grouped_g[g, h] = dst

        def quantize_g(g, h):
            nc.vector.quantize_mx(out=g_codes[g, h][:].bitcast(FP8X4), scales=g_scales[g, h][:], in_=grouped_g[g, h][:])

        def moving(w, g, h):
            if w == "z":
                return z_codes[h][:, g, :].bitcast(FP4X4), z_scales[h][:, g, :]
            if w == "r":
                return r_codes[h][:, g, :].bitcast(FP8X4), r_scales[:, g, h * NH : (h + 1) * NH]
            return g_codes[g, h][:].bitcast(FP8X4), g_scales[g, h][:]

        def multiply(w, m, h, cols=slice(0, NH)):
            bank = next_bank()
            j, t = divmod(m, 2)
            for g in range(G):
                chunk, s = ((j, 0), t) if g == 0 else ((j, 1 + t), g - 1)
                codes, scales = moving(w, g, h)
                nc.tensor.matmul_mx(
                    out=bank[:, cols],
                    lhsT=i_codes[chunk][:, s, :].bitcast(FP8X4),
                    lhsT_scale=i_scales[chunk][:, s, :],
                    rhs=codes[:, cols],
                    rhs_scale=scales[:, cols],
                    start=(g == 0),
                    stop=(g == G - 1),
                )
            sums[w, m, h] = bank

        def shift(d_sb, m, h):
            return d_sb[m // 2][:, m % 2, h * NH : (h + 1) * NH]

        def finish_z(m, h):
            nc.vector.tensor_tensor(out=acc[m, h][:], in0=sums["z", m, h][:], in1=shift(dz_sb, m, h), op=MULT)

        def finish_r(m, h):
            prod = ring.tile([P, NH], F32, name="product", bufs=9)
            nc.vector.tensor_tensor(out=prod[:], in0=sums["r", m, h][:], in1=shift(dr_sb, m, h), op=MULT)
            nc.gpsimd.tensor_tensor(out=acc[m, h][:], in0=acc[m, h][:], in1=prod[:], op=ADD)

        def finish_p(m, h, cols=slice(0, NH)):
            part = acc[m, h][:, cols]
            nc.vector.tensor_tensor(out=part, in0=sums["p", m, h][:, cols], in1=part, op=ADD)
            nc.sync.dma_start(out=out_v[:, m, h * NH + cols.start : h * NH + cols.stop], in_=part)

        nc.vector.memset(warm[:], 0.0)
        nc.vector.memset(z_scales[0][:].bitcast(I32), 0)
        nc.vector.memset(z_scales[1][:].bitcast(I32), 0)
        nc.vector.memset(r_scales[:].bitcast(I32), 0)
        nc.scalar.copy(out=warm[:, 8:9], in_=warm[:, 0:1])
        make_identity(nc, ident[:])

        load_pair(0)
        load_z(0)
        load_pair(1)
        load_z(1)
        load_d(dz_sb, dz_v, 0)
        load_pair(2)
        load_d(dz_sb, dz_v, 1)
        load_pair(3)
        load_d(dz_sb, dz_v, 2)
        load_g(0)
        load_r_scales()
        load_d(dz_sb, dz_v, 3)
        load_r(0)
        load_d(dr_sb, dr_v, 0)
        load_g(1)
        load_d(dr_sb, dr_v, 1)
        load_d(dr_sb, dr_v, 2)
        load_r(1)
        load_d(dr_sb, dr_v, 3)
        load_g(2)

        for j in range(PAIRS):
            for x in range(3):
                transpose_chunk(j, x)
            for x in range(3):
                evacuate(j, x)
            if j + 1 < PAIRS:
                for x in range(3):
                    sort_words(j + 1, x)
            for x in range(3):
                quantize_i(j, x)
            if j == 1:
                finish_z(0, 0)
                finish_z(1, 0)
            if j > 0:
                for m in (2 * j - 2, 2 * j - 1):
                    multiply("z", m, 1)
                    finish_z(m, 1)
            for m in (2 * j, 2 * j + 1):
                multiply("z", m, 0)
                if j > 0:
                    finish_z(m, 0)
        interleave_g(0, 0)
        quantize_g(0, 0)
        for m in (TILES - 2, TILES - 1):
            multiply("z", m, 1)
            finish_z(m, 1)

        after_r = {1: (0, 1), 4: (1, 0), 7: (1, 1), 11: (2, 0)}
        units = [(m, h) for h in range(HALVES) for m in range(TILES)]
        for index, (m, h) in enumerate(units):
            multiply("r", m, h)
            finish_r(m, h)
            if index in after_r:
                interleave_g(*after_r[index])
                quantize_g(*after_r[index])
        for index, (m, h) in enumerate(units[:-1]):
            multiply("p", m, h)
            finish_p(m, h)
            if index == 1:
                interleave_g(2, 1)
                quantize_g(2, 1)
        for cols in (slice(0, NH // 2), slice(NH // 2, NH)):
            multiply("p", TILES - 1, HALVES - 1, cols)
            finish_p(TILES - 1, HALVES - 1, cols)
